import numpy as np
import ml_dtypes


def mxq(x, axis, fmt="e4m3"):
    dtype, down = {"e4m3": (ml_dtypes.float8_e4m3fn, 7), "e5m2": (ml_dtypes.float8_e5m2, 14)}[fmt]
    v = np.moveaxis(np.asarray(x, np.float32).astype(ml_dtypes.bfloat16).astype(np.float64), axis, -1)
    blocks = v.reshape(v.shape[:-1] + (-1, 32))
    amax = np.abs(blocks).max(-1, keepdims=True)
    byte = np.maximum(np.where(amax > 0, np.frexp(amax)[1] - 1 + 127, 0) - down, 1)
    scale = np.exp2(byte - 127.0)
    codes = (blocks / scale).astype(np.float32).astype(dtype).astype(np.float64)
    return np.moveaxis((codes * scale).reshape(v.shape), -1, axis)


WIDE = False


def mx_kscale(k):
    if not WIDE:
        return np.ones(k)
    levels = np.array([30, -30])
    if k % 512:
        return np.exp2(np.random.permutation(np.resize(levels, k // 32))).repeat(32)
    a = np.empty((k // 512, 16))
    for p in range(k // 512):
        a[p, :8] = np.random.permutation(np.resize(levels, 8))
        for g in range(8):
            far = levels[np.abs(levels - a[p, g]) >= 10]
            a[p, g + 8] = far[np.random.randint(len(far))]
    return np.exp2(a.ravel()).repeat(32)


def f64(x):
    return np.asarray(x).astype(np.float64)


def striped(idx):
    return np.tile(np.asarray(idx).reshape(-1, 16).T, (8, 1)).astype(np.uint16)


def unstriped(offs):
    return offs[:16].T.reshape(-1).astype(np.int64)


E2M1 = np.array([0.0, 0.5, 1.0, 1.5, 2.0, 3.0, 4.0, 6.0, -0.0, -0.5, -1.0, -1.5, -2.0, -3.0, -4.0, -6.0])


def pack_weight(w, fmt):
    k, n = w.shape
    w = f64(np.asarray(w, np.float32).astype(ml_dtypes.bfloat16)).reshape(k // 32, 32, n)
    amax = np.abs(w).max(1)
    if fmt in ("e4m3", "e5m2"):
        byte = np.frexp(amax)[1] - 1 + 127 - (7 if fmt == "e4m3" else 14)
    else:
        mant, ex = np.frexp(amax / 6.0)
        byte = np.where(mant > 0.5, ex, ex - 1) + 127
    byte = np.clip(np.where(amax > 0, byte, 1), 1, 254)
    scaled = (w * np.exp2(127.0 - byte)[:, None, :]).reshape(k, n).astype(np.float32)
    by_word = np.ascontiguousarray(scaled.reshape(k // 512, 128, 4, n).transpose(0, 1, 3, 2))
    if fmt in ("e4m3", "e5m2"):
        words = by_word.astype(ml_dtypes.float8_e4m3fn if fmt == "e4m3" else ml_dtypes.float8_e5m2).view(np.uint8)
    else:
        c = by_word.astype(ml_dtypes.float4_e2m1fn).view(np.uint8) & 0xF
        words = (c[..., 0::2] | (c[..., 1::2] << 4)).reshape(k // 512, 128, 2 * n)
    return np.ascontiguousarray(words), np.ascontiguousarray(byte.astype(np.uint8).reshape(k // 512, 16, n))


def unpack_weight(words, scales, fmt):
    g, _, n = scales.shape
    words = np.ascontiguousarray(words).reshape(g, 128, n, -1)
    if fmt in ("e4m3", "e5m2"):
        vals = words.view(ml_dtypes.float8_e4m3fn if fmt == "e4m3" else ml_dtypes.float8_e5m2).astype(np.float64)
    else:
        nib = np.empty((g, 128, n, 4), np.uint8)
        nib[..., 0::2] = words & 0xF
        nib[..., 1::2] = words >> 4
        vals = E2M1[nib]
    vals = vals * np.repeat(np.exp2(scales.astype(np.float64) - 127.0), 8, axis=1)[..., None]
    return vals.transpose(0, 1, 3, 2).reshape(g * 512, n)


K, T, J, R, O, N, E = 512, 1024, 256, 512, 128, 256, 512


def setup_inputs():
    n = np.random.standard_normal
    idx = np.random.permutation(T)[:J]
    idx2 = np.random.permutation(J)[:O]
    idx3 = np.random.permutation(J)[:O]
    idx4 = np.random.permutation(J)[:O]
    idx5 = np.random.permutation(T)[:O]
    idx6 = np.random.permutation(E)[:O]
    idx7 = np.random.permutation(E)[:O]
    fk = mx_kscale(K)
    fr = mx_kscale(R)
    xtp = pack_weight(n((K, T)) / fk[:, None], "e2m1")
    wp = pack_weight(n((K, R)) * 1 / np.sqrt(K) * fk[:, None] * fr, "e4m3")
    w2p = pack_weight(n((K, R)) * 1 / np.sqrt(K) * fk[:, None], "e5m2")
    wbp = pack_weight(n((R, N)) * 1 / np.sqrt(R) / fr[:, None], "e2m1")
    wsp = pack_weight(n((K, N)) * 1 / np.sqrt(K) * fk[:, None], "e4m3")
    return {
        "xt_words": xtp[0],
        "xt_scales": xtp[1],
        "w_words": wp[0],
        "w_scales": wp[1],
        "w2_words": w2p[0],
        "w2_scales": w2p[1],
        "wb_words": wbp[0],
        "wb_scales": wbp[1],
        "ws_words": wsp[0],
        "ws_scales": wsp[1],
        "offs": striped(idx),
        "offs2": striped(idx2),
        "offs3": striped(idx3),
        "offs4": striped(idx4),
        "offs5": striped(idx5),
        "offs6": striped(idx6),
        "offs7": striped(idx7),
    }


def reference(xt_words, xt_scales, w_words, w_scales, w2_words, w2_scales, wb_words, wb_scales, ws_words, ws_scales, offs, offs2, offs3, offs4, offs5, offs6, offs7):
    idx = unstriped(offs)
    idx2 = unstriped(offs2)
    idx3 = unstriped(offs3)
    idx4 = unstriped(offs4)
    idx5 = unstriped(offs5)
    idx6 = unstriped(offs6)
    idx7 = unstriped(offs7)
    xtu = unpack_weight(xt_words, xt_scales, "e2m1")
    wu = unpack_weight(w_words, w_scales, "e4m3")
    w2u = unpack_weight(w2_words, w2_scales, "e5m2")
    wbu = unpack_weight(wb_words, wb_scales, "e2m1")
    wsu = unpack_weight(ws_words, ws_scales, "e4m3")
    xtidxg = xtu[:, idx]
    a = wu.T @ xtidxg
    b = w2u.T @ xtidxg
    lb = b[:, 0:1]
    lb2 = b[:, 128:129]
    la = a[:, 0:1]
    hid = np.maximum(a[:, idx2] * lb, a[:, idx3] * lb2) - b[:, idx4] * la
    hidq = mxq(hid, 0, "e5m2")
    xtidx5g = xtu[:, idx5]
    p = wbu.T @ hidq + wsu.T @ xtidx5g
    pa = np.zeros((N, E))
    pa[:, idx6] = p
    pb = np.zeros((N, E))
    pb[:, idx7] = p
    y = pa + pb
    return y

@@ -1,0 +1,171 @@
+from contextlib import ExitStack
+
+import concourse.mybir as mybir
+
+F32 = mybir.dt.float32
+BF16 = mybir.dt.bfloat16
+I32 = mybir.dt.int32
+U32 = mybir.dt.uint32
+U16 = mybir.dt.uint16
+U8 = mybir.dt.uint8
+E4M3 = mybir.dt.float8_e4m3fn_x4
+E5M2 = mybir.dt.float8_e5m2_x4
+E2M1 = mybir.dt.float4_e2m1fn_x4
+COPY = mybir.ActivationFunctionType.Copy
+ALU = mybir.AluOpType
+
+K, T, J, R, O, N, E = 512, 1024, 256, 512, 128, 256, 512
+P = 128
+FLOPS = 2 * K * R * J * 2 + 2 * R * N * O + 2 * K * N * O
+
+
+def tile_list_leadthree_twow_further_pagetwice_kernel(
+    tc, xt_words, xt_scales, w_words, w_scales, w2_words, w2_scales, wb_words, wb_scales, ws_words, ws_scales,
+    offs, offs2, offs3, offs4, offs5, offs6, offs7, out,
+):
+    nc = tc.nc
+    with ExitStack() as ctx:
+        keep = ctx.enter_context(tc.tile_pool(name="keep", bufs=1))
+        psum = ctx.enter_context(tc.psum_pool(name="psum", bufs=1))
+
+        def sb(name, shape, dtype):
+            return keep.tile(shape, dtype, name=name, align_bytes=64)
+
+        def load_list(name, src):
+            lst = keep.tile(list(src.shape), U16, name=name)
+            nc.sync.dma_start(lst[:], src)
+            return lst
+
+        def load_words(name, src, shape, dtype):
+            tl = sb(name, shape, dtype)
+            nc.sync.dma_start(tl[:].bitcast(I32), src.bitcast(I32))
+            return tl
+
+        def load_plane(plane, src):
+            for q in range(4):
+                nc.sync.dma_start(plane[32 * q : 32 * q + 4, :].bitcast(I32), src[0, 4 * q : 4 * q + 4, :].bitcast(I32))
+
+        x_plane = sb("x_plane", [P, T], U8)
+        stage = sb("stage", [P, 2, 2 * R], U8)
+        ws_plane = sb("ws_plane", [P, N], U8)
+        wb_plane = sb("wb_plane", [P, N], U8)
+        nc.vector.memset(x_plane[:].bitcast(I32), 0)
+        nc.vector.memset(stage[:].rearrange("p h c -> p (h c)").bitcast(I32), 0)
+        nc.vector.memset(ws_plane[:].bitcast(I32), 0)
+        nc.vector.memset(wb_plane[:].bitcast(I32), 0)
+        pages = [[sb("page%d%d" % (s, h), [P, E], F32) for h in range(2)] for s in range(2)]
+        for s in range(2):
+            for h in range(2):
+                nc.vector.memset(pages[s][h][:], 0.0)
+
+        x_words = load_words("x_words", xt_words[0], [P, T], U16)
+        l1 = load_list("l1", offs)
+        load_plane(x_plane, xt_scales)
+        raw = [
+            load_words("raw%d" % i, src[0].rearrange("p c t -> p (c t)"), [P, R], U32)
+            for i, src in enumerate((w_words, w2_words))
+        ]
+        for i, src in enumerate((w_scales, w2_scales)):
+            rows = src[0].rearrange("(h q r) c -> q r h c", h=2, q=2)
+            for q in range(2):
+                nc.sync.dma_start(stage[32 * q : 32 * q + 4, :, i * R : (i + 1) * R].bitcast(I32), rows[q].bitcast(I32))
+        l2 = load_list("l2", offs2)
+        l3 = load_list("l3", offs3)
+        l4 = load_list("l4", offs4)
+        l5 = load_list("l5", offs5)
+        ws_codes = load_words("ws_codes", ws_words[0].rearrange("p c t -> p (c t)"), [P, N], U32)
+        load_plane(ws_plane, ws_scales)
+        wb_codes = load_words("wb_codes", wb_words[0], [P, 2 * N], U8)
+        load_plane(wb_plane, wb_scales)
+        l6 = load_list("l6", offs6)
+        l7 = load_list("l7", offs7)
+
+        xg_plane = sb("xg_plane", [P, J], U8)
+        xg_words = sb("xg_words", [P, J], U16)
+        nc.vector.tensor_copy(xg_plane[:], x_plane[:].indirect(l1[:]))
+        nc.vector.tensor_copy(xg_words[:], x_words[:].indirect(l1[:]))
+
+        codes = [sb("codes%d" % i, [P, R], U32) for i in range(2)]
+        planes = [sb("planes%d" % i, [P, R], U8) for i in range(2)]
+        nc.scalar.copy(
+            codes[0][:].rearrange("p (t c i) -> p c t i", t=4, i=4),
+            raw[0][:].rearrange("p (c i t) -> p c t i", t=4, i=4),
+        )
+        nc.scalar.copy(
+            codes[1][:].rearrange("p (t c i) -> p c t i", t=4, i=4),
+            raw[1][:].rearrange("p (c i t) -> p c t i", t=4, i=4),
+        )
+        nc.vector.tensor_copy(stage[64:128, 0, :].bitcast(I32), stage[0:64, 1, :].bitcast(I32))
+        for i in range(2):
+            nc.vector.tensor_copy(
+                planes[i][:].rearrange("p (t m) -> p t m", t=4),
+                stage[:, 0, i * R : (i + 1) * R].rearrange("p (m t) -> p t m", t=4),
+            )
+
+        fmts = (E4M3, E5M2)
+        rows_ab = []
+        for t in range(4):
+            pair = []
+            for i in range(2):
+                acc = psum.tile([P, J], F32, name="acc%d%d" % (t, i), tag="bank%d" % (2 * t + i))
+                cols = slice(t * P, (t + 1) * P)
+                nc.tensor.matmul_mx(
+                    acc[:], lhsT=codes[i][:, cols].bitcast(fmts[i]), lhsT_scale=planes[i][:, cols],
+                    rhs=xg_words[:].bitcast(E2M1), rhs_scale=xg_plane[:], start=True, stop=True,
+                )
+                res = sb("res%d%d" % (t, i), [P, J], F32)
+                if t == 0 and i == 0:
+                    nc.scalar.activation(res[:], acc[:], COPY)
+                else:
+                    nc.vector.tensor_copy(res[:], acc[:])
+                pair.append(res)
+            rows_ab.append(pair)
+
+        hid = sb("hid", [P, O, 4], BF16)
+        for u in range(2):
+            g2 = sb("g2_%d" % u, [P, 2, O], F32)
+            g3 = sb("g3_%d" % u, [P, 2, O], F32)
+            g4 = sb("g4_%d" % u, [P, 2, O], F32)
+            top = sb("top_%d" % u, [P, 2, O], F32)
+            for v in range(2):
+                a, b = rows_ab[2 * u + v]
+                nc.scalar.activation(g2[:, v, :], a[:].indirect(l2[:]), COPY, scale=b[:, 0:1])
+                nc.scalar.activation(g3[:, v, :], a[:].indirect(l3[:]), COPY, scale=b[:, 128:129])
+                nc.scalar.activation(g4[:, v, :], b[:].indirect(l4[:]), COPY, scale=a[:, 0:1])
+                nc.vector.tensor_tensor(top[:, v, :], g2[:, v, :], g3[:, v, :], ALU.max)
+            nc.vector.tensor_tensor(
+                hid[:, :, 2 * u : 2 * u + 2], top[:].rearrange("p v o -> p o v"), g4[:].rearrange("p v o -> p o v"), ALU.subtract
+            )
+
+        x5_plane = sb("x5_plane", [P, O], U8)
+        x5_words = sb("x5_words", [P, O], U16)
+        nc.vector.tensor_copy(x5_plane[:], x_plane[:].indirect(l5[:]))
+        nc.vector.tensor_copy(x5_words[:], x_words[:].indirect(l5[:]))
+
+        hid_codes = sb("hid_codes", [P, O], U32)
+        hid_plane = sb("hid_plane", [P, O], U8)
+        nc.vector.quantize_mx(hid_codes[:].bitcast(E5M2), hid_plane[:], hid[:].rearrange("p o t -> p (o t)"))
+
+        accs = [psum.tile([P, O], F32, name="p%d" % h, tag="bank%d" % h) for h in range(2)]
+        for h in range(2):
+            cols = slice(h * P, (h + 1) * P)
+            nc.tensor.matmul_mx(
+                accs[h][:], lhsT=ws_codes[:, cols].bitcast(E4M3), lhsT_scale=ws_plane[:, cols],
+                rhs=x5_words[:].bitcast(E2M1), rhs_scale=x5_plane[:], start=True, stop=False,
+            )
+        for h in range(2):
+            cols = slice(h * P, (h + 1) * P)
+            nc.tensor.matmul_mx(
+                accs[h][:], lhsT=wb_codes[:, 2 * h * P : 2 * (h + 1) * P].bitcast(E2M1), lhsT_scale=wb_plane[:, cols],
+                rhs=hid_codes[:].bitcast(E5M2), rhs_scale=hid_plane[:], start=False, stop=True,
+            )
+        ps = [sb("ps%d" % h, [P, O], F32) for h in range(2)]
+        for h in range(2):
+            nc.vector.tensor_copy(ps[h][:], accs[h][:])
+        for h in range(2):
+            nc.scalar.activation(pages[1][h][:].indirect(l7[:]), ps[h][:], COPY)
+            nc.vector.tensor_copy(pages[0][h][:].indirect(l6[:]), ps[h][:])
+        for h in range(2):
+            total = sb("total%d" % h, [P, E], F32)
+            nc.vector.tensor_tensor(total[:], pages[0][h][:], pages[1][h][:], ALU.add)
+            nc.sync.dma_start(out[h * P : (h + 1) * P, :], total[:])

@@ -46,11 +46,12 @@ def tile_list_leadthree_twow_further_pagetwice_kernel(
                 nc.sync.dma_start(plane[32 * q : 32 * q + 4, :].bitcast(I32), src[0, 4 * q : 4 * q + 4, :].bitcast(I32))
 
         x_plane = sb("x_plane", [P, T], U8)
-        stage = sb("stage", [P, 2, 2 * R], U8)
+        stage = sb("stage", [4, 4, 2 * R], U8)
+        spread = sb("spread", [P, 2 * R], U8)
         ws_plane = sb("ws_plane", [P, N], U8)
         wb_plane = sb("wb_plane", [P, N], U8)
         nc.vector.memset(x_plane[:].bitcast(I32), 0)
-        nc.vector.memset(stage[:].rearrange("p h c -> p (h c)").bitcast(I32), 0)
+        nc.vector.memset(spread[:].bitcast(I32), 0)
         nc.vector.memset(ws_plane[:].bitcast(I32), 0)
         nc.vector.memset(wb_plane[:].bitcast(I32), 0)
         pages = [[sb("page%d%d" % (s, h), [P, E], F32) for h in range(2)] for s in range(2)]
@@ -58,17 +59,16 @@ def tile_list_leadthree_twow_further_pagetwice_kernel(
             for h in range(2):
                 nc.vector.memset(pages[s][h][:], 0.0)
 
-        x_words = load_words("x_words", xt_words[0], [P, T], U16)
         l1 = load_list("l1", offs)
-        load_plane(x_plane, xt_scales)
+        for i, src in enumerate((w_scales, w2_scales)):
+            rows = src[0].rearrange("(q r) c -> r q c", q=4)
+            nc.sync.dma_start(stage[:, :, i * R : (i + 1) * R].bitcast(I32), rows.bitcast(I32))
+        x_words = load_words("x_words", xt_words[0], [P, T], U16)
         raw = [
             load_words("raw%d" % i, src[0].rearrange("p c t -> p (c t)"), [P, R], U32)
             for i, src in enumerate((w_words, w2_words))
         ]
-        for i, src in enumerate((w_scales, w2_scales)):
-            rows = src[0].rearrange("(h q r) c -> q r h c", h=2, q=2)
-            for q in range(2):
-                nc.sync.dma_start(stage[32 * q : 32 * q + 4, :, i * R : (i + 1) * R].bitcast(I32), rows[q].bitcast(I32))
+        load_plane(x_plane, xt_scales)
         l2 = load_list("l2", offs2)
         l3 = load_list("l3", offs3)
         l4 = load_list("l4", offs4)
@@ -80,48 +80,44 @@ def tile_list_leadthree_twow_further_pagetwice_kernel(
         l6 = load_list("l6", offs6)
         l7 = load_list("l7", offs7)
 
+        for q in range(4):
+            nc.vector.tensor_copy(spread[32 * q : 32 * q + 4, :].bitcast(I32), stage[:, q, :].bitcast(I32))
         xg_plane = sb("xg_plane", [P, J], U8)
         xg_words = sb("xg_words", [P, J], U16)
-        nc.vector.tensor_copy(xg_plane[:], x_plane[:].indirect(l1[:]))
-        nc.vector.tensor_copy(xg_words[:], x_words[:].indirect(l1[:]))
 
         codes = [sb("codes%d" % i, [P, R], U32) for i in range(2)]
-        planes = [sb("planes%d" % i, [P, R], U8) for i in range(2)]
-        nc.scalar.copy(
-            codes[0][:].rearrange("p (t c i) -> p c t i", t=4, i=4),
-            raw[0][:].rearrange("p (c i t) -> p c t i", t=4, i=4),
-        )
-        nc.scalar.copy(
-            codes[1][:].rearrange("p (t c i) -> p c t i", t=4, i=4),
-            raw[1][:].rearrange("p (c i t) -> p c t i", t=4, i=4),
-        )
-        nc.vector.tensor_copy(stage[64:128, 0, :].bitcast(I32), stage[0:64, 1, :].bitcast(I32))
         for i in range(2):
-            nc.vector.tensor_copy(
-                planes[i][:].rearrange("p (t m) -> p t m", t=4),
-                stage[:, 0, i * R : (i + 1) * R].rearrange("p (m t) -> p t m", t=4),
+            nc.scalar.copy(
+                codes[i][:].rearrange("p (t c i) -> p c t i", t=4, i=4),
+                raw[i][:].rearrange("p (c i t) -> p c t i", t=4, i=4),
             )
+        by_t = spread[:].rearrange("p (m t) -> p t m", t=4)
+        plane_first = sb("plane_first", [P, 1, 2 * P], U8)
+        plane_rest = sb("plane_rest", [P, 3, 2 * P], U8)
+        nc.vector.tensor_copy(plane_first[:], by_t[:, 0:1, :])
+        nc.vector.tensor_copy(xg_words[:], x_words[:].indirect(l1[:]))
+        nc.vector.tensor_copy(xg_plane[:], x_plane[:].indirect(l1[:]))
+        nc.vector.tensor_copy(plane_rest[:], by_t[:, 1:4, :])
+        planes = [plane_first[:, 0, :]] + [plane_rest[:, t, :] for t in range(3)]
 
         fmts = (E4M3, E5M2)
-        rows_ab = []
-        for t in range(4):
-            pair = []
-            for i in range(2):
-                acc = psum.tile([P, J], F32, name="acc%d%d" % (t, i), tag="bank%d" % (2 * t + i))
-                cols = slice(t * P, (t + 1) * P)
-                nc.tensor.matmul_mx(
-                    acc[:], lhsT=codes[i][:, cols].bitcast(fmts[i]), lhsT_scale=planes[i][:, cols],
-                    rhs=xg_words[:].bitcast(E2M1), rhs_scale=xg_plane[:], start=True, stop=True,
-                )
-                res = sb("res%d%d" % (t, i), [P, J], F32)
-                if t == 0 and i == 0:
-                    nc.scalar.activation(res[:], acc[:], COPY)
-                else:
-                    nc.vector.tensor_copy(res[:], acc[:])
-                pair.append(res)
-            rows_ab.append(pair)
+        rows_ab = [[sb("res%d%d" % (t, i), [P, J], F32) for i in range(2)] for t in range(4)]
+        passes = [(0, 1, 0, P), (0, 0, 0, P), (0, 0, P, J), (0, 1, P, J)]
+        passes = passes + [(t, i, 0, J) for t in range(1, 4) for i in range(2)]
+        for n, (t, i, lo, hi) in enumerate(passes):
+            acc = psum.tile([P, hi - lo], F32, name="acc%d" % n, tag="bank%d" % (n % 8))
+            nc.tensor.matmul_mx(
+                acc[:], lhsT=codes[i][:, t * P : (t + 1) * P].bitcast(fmts[i]), lhsT_scale=planes[t][:, i * P : (i + 1) * P],
+                rhs=xg_words[:, lo:hi].bitcast(E2M1), rhs_scale=xg_plane[:, lo:hi], start=True, stop=True,
+            )
+            if n == 2:
+                nc.scalar.activation(rows_ab[t][i][:, lo:hi], acc[:], COPY)
+            else:
+                nc.vector.tensor_copy(rows_ab[t][i][:, lo:hi], acc[:])
 
         hid = sb("hid", [P, O, 4], BF16)
+        hid_codes = sb("hid_codes", [P, O], U32)
+        hid_plane = sb("hid_plane", [P, O], U8)
         for u in range(2):
             g2 = sb("g2_%d" % u, [P, 2, O], F32)
             g3 = sb("g3_%d" % u, [P, 2, O], F32)
@@ -142,11 +138,9 @@ def tile_list_leadthree_twow_further_pagetwice_kernel(
         nc.vector.tensor_copy(x5_plane[:], x_plane[:].indirect(l5[:]))
         nc.vector.tensor_copy(x5_words[:], x_words[:].indirect(l5[:]))
 
-        hid_codes = sb("hid_codes", [P, O], U32)
-        hid_plane = sb("hid_plane", [P, O], U8)
         nc.vector.quantize_mx(hid_codes[:].bitcast(E5M2), hid_plane[:], hid[:].rearrange("p o t -> p (o t)"))
 
-        accs = [psum.tile([P, O], F32, name="p%d" % h, tag="bank%d" % h) for h in range(2)]
+        accs = [psum.tile([P, O], F32, name="p%d" % h, tag="bank%d" % (2 + h)) for h in range(2)]
         for h in range(2):
             cols = slice(h * P, (h + 1) * P)
             nc.tensor.matmul_mx(
@@ -160,12 +154,16 @@ def tile_list_leadthree_twow_further_pagetwice_kernel(
                 rhs=hid_codes[:].bitcast(E5M2), rhs_scale=hid_plane[:], start=False, stop=True,
             )
         ps = [sb("ps%d" % h, [P, O], F32) for h in range(2)]
+        nc.vector.tensor_copy(ps[0][:], accs[0][:])
+        nc.scalar.activation(ps[1][:], accs[1][:], COPY)
         for h in range(2):
-            nc.vector.tensor_copy(ps[h][:], accs[h][:])
-        for h in range(2):
-            nc.scalar.activation(pages[1][h][:].indirect(l7[:]), ps[h][:], COPY)
             nc.vector.tensor_copy(pages[0][h][:].indirect(l6[:]), ps[h][:])
-        for h in range(2):
-            total = sb("total%d" % h, [P, E], F32)
-            nc.vector.tensor_tensor(total[:], pages[0][h][:], pages[1][h][:], ALU.add)
-            nc.sync.dma_start(out[h * P : (h + 1) * P, :], total[:])
+            nc.scalar.activation(pages[1][h][:].indirect(l7[:]), ps[h][:], COPY)
+        total = sb("total0", [P, E], F32)
+        nc.vector.tensor_tensor(total[:], pages[0][0][:], pages[1][0][:], ALU.add)
+        nc.sync.dma_start(out[0:P, :], total[:])
+        for c, queue in enumerate((nc.sync, nc.scalar)):
+            cols = slice(c * 256, (c + 1) * 256)
+            part = sb("part%d" % c, [P, 256], F32)
+            nc.vector.tensor_tensor(part[:], pages[0][1][:, cols], pages[1][1][:, cols], ALU.add)
+            queue.dma_start(out[P : 2 * P, cols], part[:])

@@ -57,7 +57,7 @@ def tile_list_leadthree_twow_further_pagetwice_kernel(
         pages = [[sb("page%d%d" % (s, h), [P, E], F32) for h in range(2)] for s in range(2)]
         for s in range(2):
             for h in range(2):
-                nc.vector.memset(pages[s][h][:], 0.0)
+                (nc.vector, nc.gpsimd)[h].memset(pages[s][h][:], 0.0)
 
         l1 = load_list("l1", offs)
         for i, src in enumerate((w_scales, w2_scales)):
@@ -85,29 +85,38 @@ def tile_list_leadthree_twow_further_pagetwice_kernel(
         xg_plane = sb("xg_plane", [P, J], U8)
         xg_words = sb("xg_words", [P, J], U16)
 
-        codes = [sb("codes%d" % i, [P, R], U32) for i in range(2)]
-        for i in range(2):
-            nc.scalar.copy(
-                codes[i][:].rearrange("p (t c i) -> p c t i", t=4, i=4),
-                raw[i][:].rearrange("p (c i t) -> p c t i", t=4, i=4),
-            )
         by_t = spread[:].rearrange("p (m t) -> p t m", t=4)
-        plane_first = sb("plane_first", [P, 1, 2 * P], U8)
-        plane_rest = sb("plane_rest", [P, 3, 2 * P], U8)
-        nc.vector.tensor_copy(plane_first[:], by_t[:, 0:1, :])
+
+        def deal_scales(t):
+            plane = keep.tile([P, 2 * P], U8, name="plane%d" % t, tag="plane%d" % (t % 2), align_bytes=64)
+            nc.vector.tensor_copy(plane[:], by_t[:, t, :])
+            return plane
+
+        w_codes = sb("w_codes", [P, 4, P], U32)
+        w2_first = sb("w2_first", [P, P], U32)
+        w2_rest = sb("w2_rest", [P, 3, P], U32)
+        runs = [r[:].rearrange("p (c i t) -> p c t i", t=4, i=4) for r in raw]
+        nc.scalar.copy(w_codes[:].rearrange("p t (c i) -> p c t i", i=4), runs[0])
+        nc.scalar.copy(w2_first[:].rearrange("p (c i) -> p c i", i=4), runs[1][:, :, 0, :])
+        nc.scalar.copy(w2_rest[:].rearrange("p t (c i) -> p c t i", i=4), runs[1][:, :, 1:4, :])
+        codes = [[w_codes[:, t, :] for t in range(4)], [w2_first[:]] + [w2_rest[:, t, :] for t in range(3)]]
+
+        planes = [deal_scales(0)]
         nc.vector.tensor_copy(xg_words[:], x_words[:].indirect(l1[:]))
-        nc.vector.tensor_copy(xg_plane[:], x_plane[:].indirect(l1[:]))
-        nc.vector.tensor_copy(plane_rest[:], by_t[:, 1:4, :])
-        planes = [plane_first[:, 0, :]] + [plane_rest[:, t, :] for t in range(3)]
+        planes.append(deal_scales(1))
+        for half in range(2):
+            nc.vector.tensor_copy(xg_plane[:, half * P : (half + 1) * P], x_plane[:].indirect(l1[:, 8 * half : 8 * half + 8]))
 
         fmts = (E4M3, E5M2)
         rows_ab = [[sb("res%d%d" % (t, i), [P, J], F32) for i in range(2)] for t in range(4)]
-        passes = [(0, 1, 0, P), (0, 0, 0, P), (0, 0, P, J), (0, 1, P, J)]
+        passes = [(0, i, lo, lo + P) for lo in (0, P) for i in range(2)]
         passes = passes + [(t, i, 0, J) for t in range(1, 4) for i in range(2)]
         for n, (t, i, lo, hi) in enumerate(passes):
+            if t == len(planes):
+                planes.append(deal_scales(t))
             acc = psum.tile([P, hi - lo], F32, name="acc%d" % n, tag="bank%d" % (n % 8))
             nc.tensor.matmul_mx(
-                acc[:], lhsT=codes[i][:, t * P : (t + 1) * P].bitcast(fmts[i]), lhsT_scale=planes[t][:, i * P : (i + 1) * P],
+                acc[:], lhsT=codes[i][t].bitcast(fmts[i]), lhsT_scale=planes[t][:, i * P : (i + 1) * P],
                 rhs=xg_words[:, lo:hi].bitcast(E2M1), rhs_scale=xg_plane[:, lo:hi], start=True, stop=True,
             )
             if n == 2:

@@ -59,10 +59,10 @@ def tile_list_leadthree_twow_further_pagetwice_kernel(
             for h in range(2):
                 (nc.vector, nc.gpsimd)[h].memset(pages[s][h][:], 0.0)
 
-        l1 = load_list("l1", offs)
         for i, src in enumerate((w_scales, w2_scales)):
             rows = src[0].rearrange("(q r) c -> r q c", q=4)
             nc.sync.dma_start(stage[:, :, i * R : (i + 1) * R].bitcast(I32), rows.bitcast(I32))
+        l1 = load_list("l1", offs)
         x_words = load_words("x_words", xt_words[0], [P, T], U16)
         raw = [
             load_words("raw%d" % i, src[0].rearrange("p c t -> p (c t)"), [P, R], U32)
@@ -168,11 +168,10 @@ def tile_list_leadthree_twow_further_pagetwice_kernel(
         for h in range(2):
             nc.vector.tensor_copy(pages[0][h][:].indirect(l6[:]), ps[h][:])
             nc.scalar.activation(pages[1][h][:].indirect(l7[:]), ps[h][:], COPY)
-        total = sb("total0", [P, E], F32)
-        nc.vector.tensor_tensor(total[:], pages[0][0][:], pages[1][0][:], ALU.add)
-        nc.sync.dma_start(out[0:P, :], total[:])
-        for c, queue in enumerate((nc.sync, nc.scalar)):
-            cols = slice(c * 256, (c + 1) * 256)
-            part = sb("part%d" % c, [P, 256], F32)
-            nc.vector.tensor_tensor(part[:], pages[0][1][:, cols], pages[1][1][:, cols], ALU.add)
-            queue.dma_start(out[P : 2 * P, cols], part[:])
+        for h in range(2):
+            for c in range(2):
+                cols = slice(c * 256, (c + 1) * 256)
+                part = sb("part%d%d" % (h, c), [P, 256], F32)
+                adder = nc.gpsimd if (h, c) == (0, 0) else nc.vector
+                adder.tensor_tensor(part[:], pages[0][h][:, cols], pages[1][h][:, cols], ALU.add)
+                nc.sync.dma_start(out[h * P : (h + 1) * P, cols], part[:])

@@ -16,6 +16,11 @@ ALU = mybir.AluOpType
 
 K, T, J, R, O, N, E = 512, 1024, 256, 512, 128, 256, 512
 P = 128
+SETS = 4
+QUADS = 4
+BANKS = 8
+HALF_J = J // 2
+HALF_E = E // 2
 FLOPS = 2 * K * R * J * 2 + 2 * R * N * O + 2 * K * N * O
 
 
@@ -37,141 +42,142 @@ def tile_list_leadthree_twow_further_pagetwice_kernel(
             return lst
 
         def load_words(name, src, shape, dtype):
-            tl = sb(name, shape, dtype)
-            nc.sync.dma_start(tl[:].bitcast(I32), src.bitcast(I32))
-            return tl
+            words = sb(name, shape, dtype)
+            nc.sync.dma_start(words[:].bitcast(I32), src.bitcast(I32))
+            return words
 
         def load_plane(plane, src):
-            for q in range(4):
+            for q in range(QUADS):
                 nc.sync.dma_start(plane[32 * q : 32 * q + 4, :].bitcast(I32), src[0, 4 * q : 4 * q + 4, :].bitcast(I32))
 
         x_plane = sb("x_plane", [P, T], U8)
-        stage = sb("stage", [4, 4, 2 * R], U8)
+        staged = sb("staged", [4, QUADS, 2 * R], U8)
         spread = sb("spread", [P, 2 * R], U8)
         ws_plane = sb("ws_plane", [P, N], U8)
         wb_plane = sb("wb_plane", [P, N], U8)
-        nc.vector.memset(x_plane[:].bitcast(I32), 0)
-        nc.vector.memset(spread[:].bitcast(I32), 0)
-        nc.vector.memset(ws_plane[:].bitcast(I32), 0)
-        nc.vector.memset(wb_plane[:].bitcast(I32), 0)
+        for plane in (x_plane, spread, ws_plane, wb_plane):
+            nc.vector.memset(plane[:].bitcast(I32), 0)
         pages = [[sb("page%d%d" % (s, h), [P, E], F32) for h in range(2)] for s in range(2)]
         for s in range(2):
             for h in range(2):
                 (nc.vector, nc.gpsimd)[h].memset(pages[s][h][:], 0.0)
 
         for i, src in enumerate((w_scales, w2_scales)):
-            rows = src[0].rearrange("(q r) c -> r q c", q=4)
-            nc.sync.dma_start(stage[:, :, i * R : (i + 1) * R].bitcast(I32), rows.bitcast(I32))
-        l1 = load_list("l1", offs)
+            rows = src[0].rearrange("(q r) c -> r q c", q=QUADS)
+            nc.sync.dma_start(staged[:, :, i * R : (i + 1) * R].bitcast(I32), rows.bitcast(I32))
+        list1 = load_list("list1", offs)
         x_words = load_words("x_words", xt_words[0], [P, T], U16)
         raw = [
             load_words("raw%d" % i, src[0].rearrange("p c t -> p (c t)"), [P, R], U32)
             for i, src in enumerate((w_words, w2_words))
         ]
         load_plane(x_plane, xt_scales)
-        l2 = load_list("l2", offs2)
-        l3 = load_list("l3", offs3)
-        l4 = load_list("l4", offs4)
-        l5 = load_list("l5", offs5)
+        list2 = load_list("list2", offs2)
+        list3 = load_list("list3", offs3)
+        list4 = load_list("list4", offs4)
+        list5 = load_list("list5", offs5)
         ws_codes = load_words("ws_codes", ws_words[0].rearrange("p c t -> p (c t)"), [P, N], U32)
         load_plane(ws_plane, ws_scales)
         wb_codes = load_words("wb_codes", wb_words[0], [P, 2 * N], U8)
         load_plane(wb_plane, wb_scales)
-        l6 = load_list("l6", offs6)
-        l7 = load_list("l7", offs7)
+        list6 = load_list("list6", offs6)
+        list7 = load_list("list7", offs7)
 
-        for q in range(4):
-            nc.vector.tensor_copy(spread[32 * q : 32 * q + 4, :].bitcast(I32), stage[:, q, :].bitcast(I32))
+        for q in range(QUADS):
+            nc.vector.tensor_copy(spread[32 * q : 32 * q + 4, :].bitcast(I32), staged[:, q, :].bitcast(I32))
         xg_plane = sb("xg_plane", [P, J], U8)
         xg_words = sb("xg_words", [P, J], U16)
+        spread_by_set = spread[:].rearrange("p (m t) -> p t m", t=SETS)
 
-        by_t = spread[:].rearrange("p (m t) -> p t m", t=4)
-
-        def deal_scales(t):
+        def sort_scales(t):
             plane = keep.tile([P, 2 * P], U8, name="plane%d" % t, tag="plane%d" % (t % 2), align_bytes=64)
-            nc.vector.tensor_copy(plane[:], by_t[:, t, :])
+            nc.vector.tensor_copy(plane[:], spread_by_set[:, t, :])
             return plane
 
-        w_codes = sb("w_codes", [P, 4, P], U32)
+        w_codes = sb("w_codes", [P, SETS, P], U32)
         w2_first = sb("w2_first", [P, P], U32)
-        w2_rest = sb("w2_rest", [P, 3, P], U32)
-        runs = [r[:].rearrange("p (c i t) -> p c t i", t=4, i=4) for r in raw]
+        w2_rest = sb("w2_rest", [P, SETS - 1, P], U32)
+        runs = [words[:].rearrange("p (c i t) -> p c t i", t=SETS, i=4) for words in raw]
         nc.scalar.copy(w_codes[:].rearrange("p t (c i) -> p c t i", i=4), runs[0])
         nc.scalar.copy(w2_first[:].rearrange("p (c i) -> p c i", i=4), runs[1][:, :, 0, :])
-        nc.scalar.copy(w2_rest[:].rearrange("p t (c i) -> p c t i", i=4), runs[1][:, :, 1:4, :])
-        codes = [[w_codes[:, t, :] for t in range(4)], [w2_first[:]] + [w2_rest[:, t, :] for t in range(3)]]
+        nc.scalar.copy(w2_rest[:].rearrange("p t (c i) -> p c t i", i=4), runs[1][:, :, 1:SETS, :])
+        codes = [[w_codes[:, t, :] for t in range(SETS)], [w2_first[:]] + [w2_rest[:, t, :] for t in range(SETS - 1)]]
 
-        planes = [deal_scales(0)]
-        nc.vector.tensor_copy(xg_words[:], x_words[:].indirect(l1[:]))
-        planes.append(deal_scales(1))
+        set_planes = [sort_scales(0)]
+        nc.vector.tensor_copy(xg_words[:], x_words[:].indirect(list1[:]))
+        set_planes.append(sort_scales(1))
         for half in range(2):
-            nc.vector.tensor_copy(xg_plane[:, half * P : (half + 1) * P], x_plane[:].indirect(l1[:, 8 * half : 8 * half + 8]))
+            nc.vector.tensor_copy(
+                xg_plane[:, half * HALF_J : (half + 1) * HALF_J], x_plane[:].indirect(list1[:, 8 * half : 8 * half + 8])
+            )
 
-        fmts = (E4M3, E5M2)
-        rows_ab = [[sb("res%d%d" % (t, i), [P, J], F32) for i in range(2)] for t in range(4)]
-        passes = [(0, i, lo, lo + P) for lo in (0, P) for i in range(2)]
-        passes = passes + [(t, i, 0, J) for t in range(1, 4) for i in range(2)]
-        for n, (t, i, lo, hi) in enumerate(passes):
-            if t == len(planes):
-                planes.append(deal_scales(t))
-            acc = psum.tile([P, hi - lo], F32, name="acc%d" % n, tag="bank%d" % (n % 8))
+        formats = (E4M3, E5M2)
+        results = [[sb("result%d%d" % (t, i), [P, J], F32) for i in range(2)] for t in range(SETS)]
+        passes = [(0, i, lo, lo + HALF_J) for lo in (0, HALF_J) for i in range(2)]
+        passes = passes + [(t, i, 0, J) for t in range(1, SETS) for i in range(2)]
+        for count, (t, i, lo, hi) in enumerate(passes):
+            if t == len(set_planes):
+                set_planes.append(sort_scales(t))
+            acc = psum.tile([P, hi - lo], F32, name="acc%d" % count, tag="bank%d" % (count % BANKS))
             nc.tensor.matmul_mx(
-                acc[:], lhsT=codes[i][t].bitcast(fmts[i]), lhsT_scale=planes[t][:, i * P : (i + 1) * P],
+                acc[:], lhsT=codes[i][t].bitcast(formats[i]), lhsT_scale=set_planes[t][:, i * P : (i + 1) * P],
                 rhs=xg_words[:, lo:hi].bitcast(E2M1), rhs_scale=xg_plane[:, lo:hi], start=True, stop=True,
             )
-            if n == 2:
-                nc.scalar.activation(rows_ab[t][i][:, lo:hi], acc[:], COPY)
+            if (t, i, lo) == (0, 0, HALF_J):
+                nc.scalar.activation(results[t][i][:, lo:hi], acc[:], COPY)
             else:
-                nc.vector.tensor_copy(rows_ab[t][i][:, lo:hi], acc[:])
+                nc.vector.tensor_copy(results[t][i][:, lo:hi], acc[:])
 
-        hid = sb("hid", [P, O, 4], BF16)
+        hid = sb("hid", [P, O, SETS], BF16)
         hid_codes = sb("hid_codes", [P, O], U32)
         hid_plane = sb("hid_plane", [P, O], U8)
-        for u in range(2):
-            g2 = sb("g2_%d" % u, [P, 2, O], F32)
-            g3 = sb("g3_%d" % u, [P, 2, O], F32)
-            g4 = sb("g4_%d" % u, [P, 2, O], F32)
-            top = sb("top_%d" % u, [P, 2, O], F32)
+        for pair in range(SETS // 2):
+            pick2 = sb("pick2_%d" % pair, [P, 2, O], F32)
+            pick3 = sb("pick3_%d" % pair, [P, 2, O], F32)
+            pick4 = sb("pick4_%d" % pair, [P, 2, O], F32)
+            larger = sb("larger_%d" % pair, [P, 2, O], F32)
             for v in range(2):
-                a, b = rows_ab[2 * u + v]
-                nc.scalar.activation(g2[:, v, :], a[:].indirect(l2[:]), COPY, scale=b[:, 0:1])
-                nc.scalar.activation(g3[:, v, :], a[:].indirect(l3[:]), COPY, scale=b[:, 128:129])
-                nc.scalar.activation(g4[:, v, :], b[:].indirect(l4[:]), COPY, scale=a[:, 0:1])
-                nc.vector.tensor_tensor(top[:, v, :], g2[:, v, :], g3[:, v, :], ALU.max)
+                a, b = results[2 * pair + v]
+                nc.scalar.activation(pick2[:, v, :], a[:].indirect(list2[:]), COPY, scale=b[:, 0:1])
+                nc.scalar.activation(pick3[:, v, :], a[:].indirect(list3[:]), COPY, scale=b[:, 128:129])
+                nc.scalar.activation(pick4[:, v, :], b[:].indirect(list4[:]), COPY, scale=a[:, 0:1])
+                nc.vector.tensor_tensor(larger[:, v, :], pick2[:, v, :], pick3[:, v, :], ALU.max)
             nc.vector.tensor_tensor(
-                hid[:, :, 2 * u : 2 * u + 2], top[:].rearrange("p v o -> p o v"), g4[:].rearrange("p v o -> p o v"), ALU.subtract
+                hid[:, :, 2 * pair : 2 * pair + 2],
+                larger[:].rearrange("p v o -> p o v"), pick4[:].rearrange("p v o -> p o v"), ALU.subtract,
             )
 
         x5_plane = sb("x5_plane", [P, O], U8)
         x5_words = sb("x5_words", [P, O], U16)
-        nc.vector.tensor_copy(x5_plane[:], x_plane[:].indirect(l5[:]))
-        nc.vector.tensor_copy(x5_words[:], x_words[:].indirect(l5[:]))
+        nc.vector.tensor_copy(x5_plane[:], x_plane[:].indirect(list5[:]))
+        nc.vector.tensor_copy(x5_words[:], x_words[:].indirect(list5[:]))
 
         nc.vector.quantize_mx(hid_codes[:].bitcast(E5M2), hid_plane[:], hid[:].rearrange("p o t -> p (o t)"))
 
-        accs = [psum.tile([P, O], F32, name="p%d" % h, tag="bank%d" % (2 + h)) for h in range(2)]
+        sums = [psum.tile([P, O], F32, name="sum%d" % h, tag="bank%d" % (2 + h)) for h in range(2)]
         for h in range(2):
             cols = slice(h * P, (h + 1) * P)
             nc.tensor.matmul_mx(
-                accs[h][:], lhsT=ws_codes[:, cols].bitcast(E4M3), lhsT_scale=ws_plane[:, cols],
+                sums[h][:], lhsT=ws_codes[:, cols].bitcast(E4M3), lhsT_scale=ws_plane[:, cols],
                 rhs=x5_words[:].bitcast(E2M1), rhs_scale=x5_plane[:], start=True, stop=False,
             )
         for h in range(2):
             cols = slice(h * P, (h + 1) * P)
             nc.tensor.matmul_mx(
-                accs[h][:], lhsT=wb_codes[:, 2 * h * P : 2 * (h + 1) * P].bitcast(E2M1), lhsT_scale=wb_plane[:, cols],
+                sums[h][:], lhsT=wb_codes[:, 2 * h * P : 2 * (h + 1) * P].bitcast(E2M1), lhsT_scale=wb_plane[:, cols],
                 rhs=hid_codes[:].bitcast(E5M2), rhs_scale=hid_plane[:], start=False, stop=True,
             )
-        ps = [sb("ps%d" % h, [P, O], F32) for h in range(2)]
-        nc.vector.tensor_copy(ps[0][:], accs[0][:])
-        nc.scalar.activation(ps[1][:], accs[1][:], COPY)
+
+        placed = [sb("placed%d" % h, [P, O], F32) for h in range(2)]
+        nc.vector.tensor_copy(placed[0][:], sums[0][:])
+        nc.scalar.activation(placed[1][:], sums[1][:], COPY)
         for h in range(2):
-            nc.vector.tensor_copy(pages[0][h][:].indirect(l6[:]), ps[h][:])
-            nc.scalar.activation(pages[1][h][:].indirect(l7[:]), ps[h][:], COPY)
+            nc.vector.tensor_copy(pages[0][h][:].indirect(list6[:]), placed[h][:])
+            nc.scalar.activation(pages[1][h][:].indirect(list7[:]), placed[h][:], COPY)
+
         for h in range(2):
             for c in range(2):
-                cols = slice(c * 256, (c + 1) * 256)
-                part = sb("part%d%d" % (h, c), [P, 256], F32)
-                adder = nc.gpsimd if (h, c) == (0, 0) else nc.vector
-                adder.tensor_tensor(part[:], pages[0][h][:, cols], pages[1][h][:, cols], ALU.add)
+                cols = slice(c * HALF_E, (c + 1) * HALF_E)
+                part = sb("part%d%d" % (h, c), [P, HALF_E], F32)
+                nc.vector.tensor_tensor(part[:], pages[0][h][:, cols], pages[1][h][:, cols], ALU.add)
                 nc.sync.dma_start(out[h * P : (h + 1) * P, cols], part[:])

from contextlib import ExitStack

import concourse.mybir as mybir

F32 = mybir.dt.float32
BF16 = mybir.dt.bfloat16
I32 = mybir.dt.int32
U32 = mybir.dt.uint32
U16 = mybir.dt.uint16
U8 = mybir.dt.uint8
E4M3 = mybir.dt.float8_e4m3fn_x4
E5M2 = mybir.dt.float8_e5m2_x4
E2M1 = mybir.dt.float4_e2m1fn_x4
COPY = mybir.ActivationFunctionType.Copy
ALU = mybir.AluOpType

K, T, J, R, O, N, E = 512, 1024, 256, 512, 128, 256, 512
P = 128
SETS = 4
QUADS = 4
BANKS = 8
HALF_J = J // 2
HALF_E = E // 2
FLOPS = 2 * K * R * J * 2 + 2 * R * N * O + 2 * K * N * O


def tile_list_leadthree_twow_further_pagetwice_kernel(
    tc, xt_words, xt_scales, w_words, w_scales, w2_words, w2_scales, wb_words, wb_scales, ws_words, ws_scales,
    offs, offs2, offs3, offs4, offs5, offs6, offs7, out,
):
    nc = tc.nc
    with ExitStack() as ctx:
        keep = ctx.enter_context(tc.tile_pool(name="keep", bufs=1))
        psum = ctx.enter_context(tc.psum_pool(name="psum", bufs=1))

        def sb(name, shape, dtype):
            return keep.tile(shape, dtype, name=name, align_bytes=64)

        def load_list(name, src):
            lst = keep.tile(list(src.shape), U16, name=name)
            nc.sync.dma_start(lst[:], src)
            return lst

        def load_words(name, src, shape, dtype):
            words = sb(name, shape, dtype)
            nc.sync.dma_start(words[:].bitcast(I32), src.bitcast(I32))
            return words

        def load_plane(plane, src):
            for q in range(QUADS):
                nc.sync.dma_start(plane[32 * q : 32 * q + 4, :].bitcast(I32), src[0, 4 * q : 4 * q + 4, :].bitcast(I32))

        x_plane = sb("x_plane", [P, T], U8)
        staged = sb("staged", [4, QUADS, 2 * R], U8)
        spread = sb("spread", [P, 2 * R], U8)
        ws_plane = sb("ws_plane", [P, N], U8)
        wb_plane = sb("wb_plane", [P, N], U8)
        for plane in (x_plane, spread, ws_plane, wb_plane):
            nc.vector.memset(plane[:].bitcast(I32), 0)
        pages = [[sb("page%d%d" % (s, h), [P, E], F32) for h in range(2)] for s in range(2)]
        for s in range(2):
            for h in range(2):
                (nc.vector, nc.gpsimd)[h].memset(pages[s][h][:], 0.0)

        for i, src in enumerate((w_scales, w2_scales)):
            rows = src[0].rearrange("(q r) c -> r q c", q=QUADS)
            nc.sync.dma_start(staged[:, :, i * R : (i + 1) * R].bitcast(I32), rows.bitcast(I32))
        list1 = load_list("list1", offs)
        x_words = load_words("x_words", xt_words[0], [P, T], U16)
        raw = [
            load_words("raw%d" % i, src[0].rearrange("p c t -> p (c t)"), [P, R], U32)
            for i, src in enumerate((w_words, w2_words))
        ]
        load_plane(x_plane, xt_scales)
        list2 = load_list("list2", offs2)
        list3 = load_list("list3", offs3)
        list4 = load_list("list4", offs4)
        list5 = load_list("list5", offs5)
        ws_codes = load_words("ws_codes", ws_words[0].rearrange("p c t -> p (c t)"), [P, N], U32)
        load_plane(ws_plane, ws_scales)
        wb_codes = load_words("wb_codes", wb_words[0], [P, 2 * N], U8)
        load_plane(wb_plane, wb_scales)
        list6 = load_list("list6", offs6)
        list7 = load_list("list7", offs7)

        for q in range(QUADS):
            nc.vector.tensor_copy(spread[32 * q : 32 * q + 4, :].bitcast(I32), staged[:, q, :].bitcast(I32))
        xg_plane = sb("xg_plane", [P, J], U8)
        xg_words = sb("xg_words", [P, J], U16)
        spread_by_set = spread[:].rearrange("p (m t) -> p t m", t=SETS)

        def sort_scales(t):
            plane = keep.tile([P, 2 * P], U8, name="plane%d" % t, tag="plane%d" % (t % 2), align_bytes=64)
            nc.vector.tensor_copy(plane[:], spread_by_set[:, t, :])
            return plane

        w_codes = sb("w_codes", [P, SETS, P], U32)
        w2_first = sb("w2_first", [P, P], U32)
        w2_rest = sb("w2_rest", [P, SETS - 1, P], U32)
        runs = [words[:].rearrange("p (c i t) -> p c t i", t=SETS, i=4) for words in raw]
        nc.scalar.copy(w_codes[:].rearrange("p t (c i) -> p c t i", i=4), runs[0])
        nc.scalar.copy(w2_first[:].rearrange("p (c i) -> p c i", i=4), runs[1][:, :, 0, :])
        nc.scalar.copy(w2_rest[:].rearrange("p t (c i) -> p c t i", i=4), runs[1][:, :, 1:SETS, :])
        codes = [[w_codes[:, t, :] for t in range(SETS)], [w2_first[:]] + [w2_rest[:, t, :] for t in range(SETS - 1)]]

        set_planes = [sort_scales(0)]
        nc.vector.tensor_copy(xg_words[:], x_words[:].indirect(list1[:]))
        set_planes.append(sort_scales(1))
        for half in range(2):
            nc.vector.tensor_copy(
                xg_plane[:, half * HALF_J : (half + 1) * HALF_J], x_plane[:].indirect(list1[:, 8 * half : 8 * half + 8])
            )

        formats = (E4M3, E5M2)
        results = [[sb("result%d%d" % (t, i), [P, J], F32) for i in range(2)] for t in range(SETS)]
        passes = [(0, i, lo, lo + HALF_J) for lo in (0, HALF_J) for i in range(2)]
        passes = passes + [(t, i, 0, J) for t in range(1, SETS) for i in range(2)]
        for count, (t, i, lo, hi) in enumerate(passes):
            if t == len(set_planes):
                set_planes.append(sort_scales(t))
            acc = psum.tile([P, hi - lo], F32, name="acc%d" % count, tag="bank%d" % (count % BANKS))
            nc.tensor.matmul_mx(
                acc[:], lhsT=codes[i][t].bitcast(formats[i]), lhsT_scale=set_planes[t][:, i * P : (i + 1) * P],
                rhs=xg_words[:, lo:hi].bitcast(E2M1), rhs_scale=xg_plane[:, lo:hi], start=True, stop=True,
            )
            if (t, i, lo) == (0, 0, HALF_J):
                nc.scalar.activation(results[t][i][:, lo:hi], acc[:], COPY)
            else:
                nc.vector.tensor_copy(results[t][i][:, lo:hi], acc[:])

        hid = sb("hid", [P, O, SETS], BF16)
        hid_codes = sb("hid_codes", [P, O], U32)
        hid_plane = sb("hid_plane", [P, O], U8)
        for pair in range(SETS // 2):
            pick2 = sb("pick2_%d" % pair, [P, 2, O], F32)
            pick3 = sb("pick3_%d" % pair, [P, 2, O], F32)
            pick4 = sb("pick4_%d" % pair, [P, 2, O], F32)
            larger = sb("larger_%d" % pair, [P, 2, O], F32)
            for v in range(2):
                a, b = results[2 * pair + v]
                nc.scalar.activation(pick2[:, v, :], a[:].indirect(list2[:]), COPY, scale=b[:, 0:1])
                nc.scalar.activation(pick3[:, v, :], a[:].indirect(list3[:]), COPY, scale=b[:, 128:129])
                nc.scalar.activation(pick4[:, v, :], b[:].indirect(list4[:]), COPY, scale=a[:, 0:1])
                nc.vector.tensor_tensor(larger[:, v, :], pick2[:, v, :], pick3[:, v, :], ALU.max)
            nc.vector.tensor_tensor(
                hid[:, :, 2 * pair : 2 * pair + 2],
                larger[:].rearrange("p v o -> p o v"), pick4[:].rearrange("p v o -> p o v"), ALU.subtract,
            )

        x5_plane = sb("x5_plane", [P, O], U8)
        x5_words = sb("x5_words", [P, O], U16)
        nc.vector.tensor_copy(x5_plane[:], x_plane[:].indirect(list5[:]))
        nc.vector.tensor_copy(x5_words[:], x_words[:].indirect(list5[:]))

        nc.vector.quantize_mx(hid_codes[:].bitcast(E5M2), hid_plane[:], hid[:].rearrange("p o t -> p (o t)"))

        sums = [psum.tile([P, O], F32, name="sum%d" % h, tag="bank%d" % (2 + h)) for h in range(2)]
        for h in range(2):
            cols = slice(h * P, (h + 1) * P)
            nc.tensor.matmul_mx(
                sums[h][:], lhsT=ws_codes[:, cols].bitcast(E4M3), lhsT_scale=ws_plane[:, cols],
                rhs=x5_words[:].bitcast(E2M1), rhs_scale=x5_plane[:], start=True, stop=False,
            )
        for h in range(2):
            cols = slice(h * P, (h + 1) * P)
            nc.tensor.matmul_mx(
                sums[h][:], lhsT=wb_codes[:, 2 * h * P : 2 * (h + 1) * P].bitcast(E2M1), lhsT_scale=wb_plane[:, cols],
                rhs=hid_codes[:].bitcast(E5M2), rhs_scale=hid_plane[:], start=False, stop=True,
            )

        placed = [sb("placed%d" % h, [P, O], F32) for h in range(2)]
        nc.vector.tensor_copy(placed[0][:], sums[0][:])
        nc.scalar.activation(placed[1][:], sums[1][:], COPY)
        for h in range(2):
            nc.vector.tensor_copy(pages[0][h][:].indirect(list6[:]), placed[h][:])
            nc.scalar.activation(pages[1][h][:].indirect(list7[:]), placed[h][:], COPY)

        for h in range(2):
            for c in range(2):
                cols = slice(c * HALF_E, (c + 1) * HALF_E)
                part = sb("part%d%d" % (h, c), [P, HALF_E], F32)
                nc.vector.tensor_tensor(part[:], pages[0][h][:, cols], pages[1][h][:, cols], ALU.add)
                nc.sync.dma_start(out[h * P : (h + 1) * P, cols], part[:])
